import numpy as np, ml_dtypes
CORES = [12,28,60,100,156,228]
N = 6
import mx_ref
NC, ROOT = 128, 5
A = np.float32(0.0125)
BF = ml_dtypes.bfloat16
def cut(t, i, w=512):
    return t[:, w * i:w * i + w]
def tile(rs):
    return np.stack(rs, axis=2).reshape(128, -1).astype(BF)
def setup_inputs(rng):
    def f(*shape):
        return mx_ref.flush((rng.standard_normal(shape, dtype=np.float32) * np.exp2(rng.integers(-2, 3, shape[:-1] + (1,)))).astype(BF))
    return {"q": f(N, 128, 4 * NC), "k": f(N, 128, 4 * 512), "v": f(N, 128, 512)}
def setup_inputs_blocks(rng):
    d = setup_inputs(rng)
    for k in ("v",): d[k] = mx_ref.spread(d[k], rng, 4)
    for k in ("q", "k"): d[k] = mx_ref.spread(d[k], rng, 1)
    return d
def setup_inputs_wide(rng):
    d = setup_inputs(rng)
    for k in ("v",): d[k] = mx_ref.flush((d[k].astype(np.float32) * np.exp2(rng.integers(-8, 9, (N, 1, 1))).astype(np.float32)).astype(BF))
    return d
def setup_inputs_sharp(rng):
    d = setup_inputs(rng); v = d["q"].astype(np.float32).reshape(N, 128, -1, 4)
    d["q"] = mx_ref.flush((v * np.exp2(rng.integers(-2, 4, (N, 1, v.shape[2], 1))).astype(np.float32)).reshape(d["q"].shape).astype(BF))
    return d
def setup_inputs_offset(rng):
    d = setup_inputs(rng); v = d["k"].astype(np.float32).reshape(N, 128, -1, 4)
    d["k"] = mx_ref.flush((v + 12 * rng.standard_normal((1, 128, 1, 4), dtype=np.float32)).reshape(d["k"].shape).astype(BF))
    return d
def reference(q, k, v, own=None):
    ONE = mx_ref.quantize(np.ones((128, 512), BF)); Q = mx_ref.quantize(q[ROOT])
    S = [[mx_ref.matmul(mx_ref.quantize(cut(k[j], b)), Q) * A for b in range(4)] for j in range(N)]
    lo = np.stack([np.max(s, axis=(0, 1))[None] for s in S]); hi = np.broadcast_to(lo.max(axis=0) + 8, lo.shape).copy()
    c = lo if own is None else own["c"]
    p = np.stack([tile([np.exp(np.maximum(s - c[j], -20).astype(np.float64)).astype(np.float32) for s in S[j]]) for j in range(N)])
    use = p if own is None else own["p"]
    e = np.exp((c - c.max(axis=0)).astype(np.float64))[:, 0]; wlo = np.zeros((N, N, NC), np.float32); whi = np.ones((N, N, NC), np.float32); wlo[ROOT] = e * (1 - 4e-5); whi[ROOT] = e * (1 + 4e-5)
    w = np.zeros((N, N, NC), np.float32); w[ROOT] = e
    if own is not None: w = own["w"]
    num = den = 0
    for j in range(N):
        P = mx_ref.quantize(use[j])
        num = num + w[ROOT][j].astype(np.float64) * mx_ref.matmul(mx_ref.quantize(v[j]), P); den = den + w[ROOT][j].astype(np.float64) * mx_ref.matmul(ONE, P)
    o = np.full((N, 128, NC), np.nan, np.float32); o[ROOT] = (num / den).astype(np.float32)
    return {"c": c, "c__lo": lo, "c__hi": hi, "p": p, "w": w, "w__lo": wlo, "w__hi": whi, "o": o}

@@ -1,0 +1,300 @@
+import numpy as np
+from concourse.bass import DstId, RemoteDMATransfer
+from concourse.mybir import dt, AluOpType, AxisListType, ActivationFunctionType
+
+NSIM = 256
+N, NQ = 6, 128
+A = float(np.float32(0.0125))
+AW, SLOT = 129, 132
+NT = 5
+F32, BF, CODE, U8 = "float32", "bfloat16", "float8_e4m3fn_x4", "uint8"
+
+SCRATCH = {
+    "qt": ("sbuf", [128, 512], BF), "kt": ("sbuf", [128, 2048], BF), "vt": ("sbuf", [128, 512], BF),
+    "onet": ("sbuf", [128, 512], BF),
+    "Qc": ("sbuf", [128, 128], CODE), "Qs": ("sbuf", [128, 128], U8),
+    "Kc": ("sbuf", [128, 512], CODE), "Ks": ("sbuf", [128, 512], U8),
+    "VOc": ("sbuf", [128, 256], CODE), "VOs": ("sbuf", [128, 256], U8),
+    "Pc": ("sbuf", [128, 128], CODE), "Ps": ("sbuf", [128, 128], U8),
+    "ps_st": ("psum", [128, 1024], F32), "ps_s": ("psum", [128, 2048], F32), "ps_al": ("psum", [128, 512], F32),
+    "atile": ("sbuf", [128, 32], F32), "n20": ("sbuf", [128, 1], F32), "fl": ("sbuf", [128, 1], BF),
+    "m2": ("sbuf", [128, 4], F32), "xe": ("sbuf", [128, 32], F32), "xt": ("sbuf", [128, 128], F32),
+    "cb": ("sbuf", [128, 128], F32), "t1": ("sbuf", [128, 512], F32), "e": ("sbuf", [128, 512], BF),
+    "pt": ("sbuf", [128, 512], BF), "snd": ("sbuf", [128, SLOT], F32),
+    "CL": ("sbuf", [128, 8], F32), "G": ("sbuf", [128, 5 * SLOT], F32),
+    "C6": ("sbuf", [128, 8], F32), "negM": ("sbuf", [128, 1], F32),
+    "W": ("sbuf", [128, 32], F32), "WT": ("sbuf", [128, 32], F32),
+    "ta": ("sbuf", [128, SLOT], F32), "tb": ("sbuf", [128, SLOT], F32),
+    "YB": ("sbuf", [128, NT * AW], F32), "RHO": ("sbuf", [128, NT * AW], F32), "Z": ("sbuf", [128, NT * AW], F32),
+    "r": ("sbuf", [128, 1], F32), "XB": ("sbuf", [128, 128], F32), "O": ("sbuf", [128, 128], F32),
+}
+SEMAPHORES = ["q", "k", "v", "one", "cst", "n20", "fl", "w0", "oneq", "qq", "vq", "kq", "qs", "qc", "loc",
+              "sta", "stb", "s0", "s1", "s2", "s3", "m0", "m1", "m2", "xe", "xt", "row", "cb",
+              "t0", "t1", "t2", "t3", "x0", "x1", "x2", "x3", "e0", "e1", "e2", "e3", "pt", "pq", "al", "snd",
+              "carr", "a0", "a1", "a2", "a3", "a4", "c6", "nm", "w", "wt", "ya", "yb", "y", "rho1", "rho2",
+              "z", "r", "xb", "o", "cout", "pout", "wout", "oout"]
+
+
+def _nb(mask):
+    return bin(mask).count("1")
+
+
+def _chip_cores(topo, c):
+    return [x for x in range(NSIM) if topo.host(x) == topo.host(c) and topo.chip(x) == topo.chip(c) and x != c]
+
+
+def _plan(T, topo):
+    cores = list(T.cores)
+    root = cores[T.root]
+    qrel, rrel = {}, {}
+    for j in range(N):
+        if j == T.root:
+            continue
+        if not topo.may_write(root, cores[j]):
+            cand = [x for x in _chip_cores(topo, root) if topo.may_write(x, cores[j])]
+            qrel[j] = cand[len(qrel) % len(cand)]
+        if not topo.may_write(cores[j], root):
+            cand = [x for x in _chip_cores(topo, cores[j]) if topo.may_write(x, root)]
+            rrel[j] = cand[(len(rrel) + len(cand) // 2) % len(cand)]
+    return qrel, rrel
+
+
+def rank_program(g, core, T, topo):
+    S = T.sem
+    cores = list(T.cores)
+    rootr = T.root
+    root = cores[rootr]
+    qrel, rrel = _plan(T, topo)
+    rank = T.rank_of(core)
+    ALU, ACTF = AluOpType, ActivationFunctionType
+    u8 = dt.uint8
+
+    def send(dst, out, in_, rsem):
+        rid, pid = topo.addr(dst, core)
+        m = topo.mask(core, dst)
+        g.remote_dma(out_ap=out, in_ap=in_, remote_sem=rsem, local_sem=S.loc, pid=pid, routing_id=rid,
+                     dma_engine_mask=m)
+        return _nb(m)
+
+    def slot(j):
+        return T.G[:, SLOT * j:SLOT * j + AW]
+
+    if rank is None:
+        loc = 0
+        mine = [j for j in qrel if qrel[j] == core]
+        if mine:
+            nin = _nb(topo.mask(root, core))
+            g.wait_ge(S.qs, nin)
+            for j in mine:
+                loc += send(cores[j], T.Qs[:], T.Qs[:], S.qs)
+            g.wait_ge(S.qc, nin)
+            for j in mine:
+                loc += send(cores[j], T.Qc[:].bitcast(u8), T.Qc[:].bitcast(u8), S.qc)
+        for j in [j for j in rrel if rrel[j] == core]:
+            nin = _nb(topo.mask(cores[j], core))
+            g.wait_ge(S.carr, nin)
+            loc += send(root, T.CL[:, j:j + 1], T.CL[:, j:j + 1], S.carr)
+            g.wait_ge(S["a%d" % j], nin)
+            loc += send(root, slot(j), slot(j), S["a%d" % j])
+        if loc:
+            g.wait_ge(S.loc, loc)
+        return
+
+    V, P, AC, SY = g.vector, g.tensor, g.scalar, g.sync
+    is_root = rank == rootr
+
+    if is_root:
+        SY.dma_start(T.qt[:], T.q[:]).then_inc(S.q, 16)
+        SY.wait_ge(S.q, 16)
+        SY.dma_start(T.kt[:], T.k[:]).then_inc(S.k, 16)
+        SY.dma_start(T.vt[:], T.v[:]).then_inc(S.v, 16)
+    else:
+        SY.dma_start(T.kt[:], T.k[:]).then_inc(S.k, 16)
+        AC.dma_start(T.vt[:], T.v[:]).then_inc(S.v, 16)
+
+    V.memset(T.onet[:], 1.0).then_inc(S.one, 1)
+    V.memset(T.atile[:], A).then_inc(S.cst, 1)
+    V.memset(T.n20[:], -20.0).then_inc(S.n20, 1)
+    V.memset(T.W[:], 0.0).then_inc(S.w0, 1)
+    if is_root:
+        V.wait_ge(S.q, 16)
+        V.quantize_mx(T.Qc[:], T.Qs[:], T.qt[:]).then_inc(S.qq, 1)
+        V.memset(T.RHO[:], 1.0).then_inc(S.rho1, 1)
+        V.wait_ge(S.rho1, 1)
+        V.tensor_scalar(T.RHO[:, 0:NT * AW:NT], T.RHO[:, 0:NT * AW:NT], 0.0, None, ALU.mult).then_inc(S.rho2, 1)
+    V.wait_ge(S.one, 1)
+    V.quantize_mx(T.VOc[:, 128:256], T.VOs[:, 128:256], T.onet[:]).then_inc(S.oneq, 1)
+    V.wait_ge(S.k, 16)
+    V.quantize_mx(T.Kc[:], T.Ks[:], T.kt[:]).then_inc(S.kq, 1)
+    V.wait_ge(S.v, 16)
+    V.quantize_mx(T.VOc[:, 0:128], T.VOs[:, 0:128], T.vt[:]).then_inc(S.vq, 1)
+
+    AC.wait_ge(S.n20, 1)
+    AC.activation(T.fl[:], T.n20[:], ACTF.Exp).then_inc(S.fl, 1)
+
+    loc = 0
+    if is_root:
+        g.wait_ge(S.qq, 1)
+        rel = [qrel[j] for j in sorted(qrel)]
+        if rel:
+            m = topo.mask(core, rel[0])
+            for x in rel:
+                m &= topo.mask(core, x)
+            ids = [DstId(rid=topo.addr(x, core)[0], pnc=topo.addr(x, core)[1]) for x in rel]
+            g.remote_dma_fused([RemoteDMATransfer(dst_ids=ids, dma_engine_mask=m, remote_sem=S.qs, srcs=[T.Qs[:]],
+                                                  dsts=[T.Qs[:] for x in rel])], local_sem=S.loc)
+            g.remote_dma_fused([RemoteDMATransfer(dst_ids=ids, dma_engine_mask=m, remote_sem=S.qc,
+                                                  srcs=[T.Qc[:].bitcast(u8)],
+                                                  dsts=[T.Qc[:].bitcast(u8) for x in rel])], local_sem=S.loc)
+            loc += 2 * _nb(m)
+        for j in range(N):
+            if j != rootr and j not in qrel:
+                loc += send(cores[j], T.Qs[:], T.Qs[:], S.qs)
+                loc += send(cores[j], T.Qc[:].bitcast(u8), T.Qc[:].bitcast(u8), S.qc)
+        P.wait_ge(S.qq, 1)
+    else:
+        nin = _nb(topo.mask(qrel.get(rank, root), core))
+        P.wait_ge(S.qs, nin)
+        P.wait_ge(S.qc, nin)
+
+    P.wait_ge(S.kq, 1)
+    P.matmul_mx(T.ps_st[:, 0:256], T.Qc[:], T.Qs[:], T.Kc[:, 0:256], T.Ks[:, 0:256], True, True).then_inc(S.sta, 1)
+    P.matmul_mx(T.ps_st[:, 512:768], T.Qc[:], T.Qs[:], T.Kc[:, 256:512], T.Ks[:, 256:512], True, True).then_inc(S.stb, 1)
+    for b in range(4):
+        P.matmul_mx(T.ps_s[:, 512 * b:512 * b + 128], T.Kc[:, 128 * b:128 * b + 128], T.Ks[:, 128 * b:128 * b + 128],
+                    T.Qc[:], T.Qs[:], True, True).then_inc(S["s%d" % b], 1)
+    for b in range(4):
+        AC.wait_ge(S["s%d" % b], 1)
+        AC.activation(T.t1[:, 128 * b:128 * b + 128], T.ps_s[:, 512 * b:512 * b + 128], ACTF.Identity,
+                      scale=A).then_inc(S["t%d" % b], 1)
+
+    V.wait_ge(S.sta, 1)
+    V.tensor_reduce(T.m2[:, 0:1], T.ps_st[:, 0:256], AxisListType.X, ALU.max).then_inc(S.m0, 1)
+    V.wait_ge(S.m0, 1)
+    V.tensor_scalar(T.m2[:, 2:3], T.m2[:, 0:1], A, None, ALU.mult).then_inc(S.m1, 1)
+    V.wait_ge(S.stb, 1)
+    V.tensor_reduce(T.m2[:, 1:2], T.ps_st[:, 512:768], AxisListType.X, ALU.max).then_inc(S.m2, 1)
+    V.wait_ge(S.m1, 1)
+    V.wait_ge(S.m2, 1)
+    V.wait_ge(S.cst, 1)
+    V.tensor_scalar(T.xe[:], T.atile[:], T.m2[:, 1:2], T.m2[:, 2:3], ALU.mult, ALU.max).then_inc(S.xe, 1)
+    V.wait_ge(S.xe, 1)
+    V.transpose(T.xt[:, 0:32], T.xe[:]).then_inc(S.xt, 1)
+    V.wait_ge(S.xt, 1)
+    for a in range(1, 4):
+        V.tensor_copy(T.xt[0:1, 32 * a:32 * a + 32], T.xt[32 * a:32 * a + 1, 0:32]).then_inc(S.row, 1)
+    g.wait_ge(S.xt, 1)
+    g.wait_ge(S.row, 3)
+    g.partition_broadcast(T.cb[:], T.xt[0:1, 0:128], 128).then_inc(S.cb, 1)
+    SY.wait_ge(S.xt, 1)
+    SY.wait_ge(S.row, 3)
+    SY.dma_start(T.c[:], T.xt[0:1, 0:128]).then_inc(S.cout, 16)
+
+    nxt = rrel.get(rank, root)
+    if not is_root:
+        g.wait_ge(S.xe, 1)
+        loc += send(nxt, T.CL[:, rank:rank + 1], T.xe[:, 0:1], S.carr)
+
+    V.wait_ge(S.cb, 1)
+    for b in range(4):
+        V.wait_ge(S["t%d" % b], 1)
+        V.tensor_tensor(T.t1[:, 128 * b:128 * b + 128], T.t1[:, 128 * b:128 * b + 128], T.cb[:],
+                        ALU.subtract).then_inc(S["x%d" % b], 1)
+        AC.wait_ge(S["x%d" % b], 1)
+        AC.activation(T.e[:, 128 * b:128 * b + 128], T.t1[:, 128 * b:128 * b + 128], ACTF.Exp).then_inc(S["e%d" % b], 1)
+    V.wait_ge(S.fl, 1)
+    for b in range(4):
+        V.wait_ge(S["e%d" % b], 1)
+        V.tensor_scalar(T.pt[:, b:512:4], T.e[:, 128 * b:128 * b + 128], T.fl[:, 0:1], None, ALU.max).then_inc(S.pt, 1)
+    V.wait_ge(S.pt, 4)
+    V.quantize_mx(T.Pc[:], T.Ps[:], T.pt[:]).then_inc(S.pq, 1)
+    SY.wait_ge(S.pt, 4)
+    SY.dma_start(T.p[:], T.pt[:]).then_inc(S.pout, 16)
+
+    P.wait_ge(S.pq, 1)
+    P.wait_ge(S.vq, 1)
+    P.wait_ge(S.oneq, 1)
+    P.matmul_mx(T.ps_al[:, 0:130], T.Pc[:], T.Ps[:], T.VOc[:, 0:130], T.VOs[:, 0:130], True, True).then_inc(S.al, 1)
+
+    if not is_root:
+        V.wait_ge(S.al, 1)
+        V.tensor_copy(T.snd[:, 0:AW], T.ps_al[:, 0:AW]).then_inc(S.snd, 1)
+        g.wait_ge(S.snd, 1)
+        loc += send(nxt, slot(rank), T.snd[:, 0:AW], S["a%d" % rank])
+        g.wait_ge(S.loc, loc)
+        SY.wait_ge(S.w0, 1)
+        for a in range(4):
+            SY.dma_start(T.w[0:N, 32 * a:32 * a + 32], T.W[0:N, 0:32]).then_inc(S.wout, 16)
+        SY.wait_ge(S.cout, 16)
+        SY.wait_ge(S.pout, 16)
+        SY.wait_ge(S.wout, 64)
+        return
+
+    others = [j for j in range(N) if j != rootr]
+    near = [j for j in others if j not in rrel]
+    far = [j for j in others if j in rrel]
+    ncarr = sum(_nb(topo.mask(rrel.get(j, cores[j]), core)) for j in others)
+    V.tensor_copy(T.C6[:, rootr:rootr + 1], T.xe[:, 0:1]).then_inc(S.c6, 1)
+    V.wait_ge(S.carr, ncarr)
+    V.tensor_copy(T.C6[:, 0:N - 1], T.CL[:, 0:N - 1]).then_inc(S.c6, 1)
+    V.wait_ge(S.c6, 2)
+    V.tensor_reduce(T.negM[:], T.C6[:, 0:N], AxisListType.X, ALU.max, negate=True).then_inc(S.nm, 1)
+    AC.wait_ge(S.nm, 1)
+    AC.wait_ge(S.c6, 2)
+    AC.wait_ge(S.w0, 1)
+    AC.activation(T.W[:, 0:N], T.C6[:, 0:N], ACTF.Exp, bias=T.negM[:, 0:1]).then_inc(S.w, 1)
+    AC.wait_ge(S.w, 1)
+    V.wait_ge(S.w, 1)
+    V.wait_ge(S.w0, 1)
+    V.transpose(T.WT[:], T.W[:]).then_inc(S.wt, 1)
+    SY.wait_ge(S.wt, 1)
+    for a in range(4):
+        SY.dma_start(T.w[0:N, 32 * a:32 * a + 32], T.WT[32 * a:32 * a + N, 0:32]).then_inc(S.wout, 16)
+
+    def arrived(q, j):
+        q.wait_ge(S["a%d" % j], _nb(topo.mask(rrel.get(j, cores[j]), core)))
+
+    V.wait_ge(S.al, 1)
+    V.tensor_scalar(T.ta[:, 0:AW], T.ps_al[:, 0:AW], T.W[:, rootr:rootr + 1], None, ALU.mult).then_inc(S.ya, 1)
+    j = near[0]
+    arrived(AC, j)
+    AC.activation(T.tb[:, 0:AW], slot(j), ACTF.Identity, scale=T.W[:, j:j + 1]).then_inc(S.yb, 1)
+    V.wait_ge(S.ya, 1)
+    V.wait_ge(S.yb, 1)
+    V.tensor_tensor(T.YB[:, 0:NT * AW:NT], T.ta[:, 0:AW], T.tb[:, 0:AW], ALU.add).then_inc(S.y, 1)
+    for i, j in enumerate(far):
+        out = T.YB[:, i + 1:NT * AW:NT]
+        if i % 2 == 0:
+            arrived(AC, j)
+            AC.activation(out, slot(j), ACTF.Identity, scale=T.W[:, j:j + 1]).then_inc(S.y, 1)
+        else:
+            arrived(V, j)
+            V.tensor_scalar(out, slot(j), T.W[:, j:j + 1], None, ALU.mult).then_inc(S.y, 1)
+    V.wait_ge(S.y, NT)
+    V.wait_ge(S.rho2, 1)
+    V.tensor_tensor_scan(T.Z[:], T.RHO[:], T.YB[:], 0.0, ALU.mult, ALU.add).then_inc(S.z, 1)
+    V.wait_ge(S.z, 1)
+    V.reciprocal(T.r[:], T.Z[:, NT * AW - 1:NT * AW]).then_inc(S.r, 1)
+    V.wait_ge(S.r, 1)
+    AC.wait_ge(S.z, 1)
+    AC.wait_ge(S.r, 1)
+    n = 0
+    for a in range(4):
+        for b in range(4):
+            in0 = T.Z[32 * a:32 * a + 32, NT * 32 * b + NT - 1:NT * 32 * (b + 1):NT]
+            out = T.XB[32 * b:32 * b + 32, 32 * a:32 * a + 32]
+            sc = T.r[32 * a:32 * a + 32, 0:1]
+            if n % 2 == 0:
+                V.tensor_scalar(out, in0, sc, None, ALU.mult).then_inc(S.xb, 1)
+            else:
+                AC.activation(out, in0, ACTF.Identity, scale=sc).then_inc(S.xb, 1)
+            n += 1
+    V.wait_ge(S.xb, 16)
+    V.transpose(T.O[:], T.XB[:]).then_inc(S.o, 1)
+    SY.wait_ge(S.o, 1)
+    SY.dma_start(T.o[:], T.O[:]).then_inc(S.oout, 16)
+    g.wait_ge(S.loc, loc)
+    SY.wait_ge(S.cout, 16)
+    SY.wait_ge(S.pout, 16)
+    SY.wait_ge(S.wout, 64)
+    SY.wait_ge(S.oout, 16)

@@ -16,10 +16,11 @@ SCRATCH = {
     "Kc": ("sbuf", [128, 512], CODE), "Ks": ("sbuf", [128, 512], U8),
     "VOc": ("sbuf", [128, 256], CODE), "VOs": ("sbuf", [128, 256], U8),
     "Pc": ("sbuf", [128, 128], CODE), "Ps": ("sbuf", [128, 128], U8),
-    "ps_st": ("psum", [128, 1024], F32), "ps_s": ("psum", [128, 2048], F32), "ps_al": ("psum", [128, 512], F32),
-    "atile": ("sbuf", [128, 32], F32), "n20": ("sbuf", [128, 1], F32), "fl": ("sbuf", [128, 1], BF),
-    "m2": ("sbuf", [128, 4], F32), "xe": ("sbuf", [128, 32], F32), "xt": ("sbuf", [128, 128], F32),
-    "cb": ("sbuf", [128, 128], F32), "t1": ("sbuf", [128, 512], F32), "e": ("sbuf", [128, 512], BF),
+    "ps_st": ("psum", [128, 1024], F32), "ps_al": ("psum", [128, 512], F32),
+    "n20": ("sbuf", [128, 1], F32), "fl": ("sbuf", [128, 1], BF),
+    "m2": ("sbuf", [128, 4], F32), "negc": ("sbuf", [128, 4], F32), "ccol": ("sbuf", [128, 4], F32),
+    "zw": ("sbuf", [128, 128], F32),
+    "e": ("sbuf", [128, 512], BF), "X": ("sbuf", [128, 512], BF),
     "pt": ("sbuf", [128, 512], BF), "snd": ("sbuf", [128, SLOT], F32),
     "CL": ("sbuf", [128, 8], F32), "G": ("sbuf", [128, 5 * SLOT], F32),
     "C6": ("sbuf", [128, 8], F32), "negM": ("sbuf", [128, 1], F32),
@@ -28,9 +29,9 @@ SCRATCH = {
     "YB": ("sbuf", [128, NT * AW], F32), "RHO": ("sbuf", [128, NT * AW], F32), "Z": ("sbuf", [128, NT * AW], F32),
     "r": ("sbuf", [128, 1], F32), "XB": ("sbuf", [128, 128], F32), "O": ("sbuf", [128, 128], F32),
 }
-SEMAPHORES = ["q", "k", "v", "one", "cst", "n20", "fl", "w0", "oneq", "qq", "vq", "kq", "qs", "qc", "loc",
-              "sta", "stb", "s0", "s1", "s2", "s3", "m0", "m1", "m2", "xe", "xt", "row", "cb",
-              "t0", "t1", "t2", "t3", "x0", "x1", "x2", "x3", "e0", "e1", "e2", "e3", "pt", "pq", "al", "snd",
+SEMAPHORES = ["q", "k", "v", "one", "n20", "fl", "w0", "oneq", "qq", "vq", "kq", "qs", "qc", "loc",
+              "sta", "stb", "m0", "m1", "nc", "cc", "zw", "tr",
+              "e0", "e1", "e2", "e3", "pt", "pq", "al", "snd",
               "carr", "a0", "a1", "a2", "a3", "a4", "c6", "nm", "w", "wt", "ya", "yb", "y", "rho1", "rho2",
               "z", "r", "xb", "o", "cout", "pout", "wout", "oout"]
 
@@ -105,23 +106,23 @@ def rank_program(g, core, T, topo):
 
     if is_root:
         SY.dma_start(T.qt[:], T.q[:]).then_inc(S.q, 16)
-        SY.wait_ge(S.q, 16)
-        SY.dma_start(T.kt[:], T.k[:]).then_inc(S.k, 16)
-        SY.dma_start(T.vt[:], T.v[:]).then_inc(S.v, 16)
     else:
         SY.dma_start(T.kt[:], T.k[:]).then_inc(S.k, 16)
         AC.dma_start(T.vt[:], T.v[:]).then_inc(S.v, 16)
 
     V.memset(T.onet[:], 1.0).then_inc(S.one, 1)
-    V.memset(T.atile[:], A).then_inc(S.cst, 1)
     V.memset(T.n20[:], -20.0).then_inc(S.n20, 1)
-    V.memset(T.W[:], 0.0).then_inc(S.w0, 1)
     if is_root:
+        V.memset(T.W[:], 0.0).then_inc(S.w0, 1)
         V.wait_ge(S.q, 16)
         V.quantize_mx(T.Qc[:], T.Qs[:], T.qt[:]).then_inc(S.qq, 1)
         V.memset(T.RHO[:], 1.0).then_inc(S.rho1, 1)
         V.wait_ge(S.rho1, 1)
         V.tensor_scalar(T.RHO[:, 0:NT * AW:NT], T.RHO[:, 0:NT * AW:NT], 0.0, None, ALU.mult).then_inc(S.rho2, 1)
+    else:
+        V.memset(T.zw[:], 0.0).then_inc(S.zw, 1)
+        SY.wait_ge(S.zw, 1)
+        SY.dma_start(T.w[:], T.zw[0:N, 0:NQ]).then_inc(S.wout, 16)
     V.wait_ge(S.one, 1)
     V.quantize_mx(T.VOc[:, 128:256], T.VOs[:, 128:256], T.onet[:]).then_inc(S.oneq, 1)
     V.wait_ge(S.k, 16)
@@ -151,6 +152,9 @@ def rank_program(g, core, T, topo):
             if j != rootr and j not in qrel:
                 loc += send(cores[j], T.Qs[:], T.Qs[:], S.qs)
                 loc += send(cores[j], T.Qc[:].bitcast(u8), T.Qc[:].bitcast(u8), S.qc)
+        SY.wait_ge(S.loc, loc)
+        SY.dma_start(T.kt[:], T.k[:]).then_inc(S.k, 16)
+        SY.dma_start(T.vt[:], T.v[:]).then_inc(S.v, 16)
         P.wait_ge(S.qq, 1)
     else:
         nin = _nb(topo.mask(qrel.get(rank, root), core))
@@ -160,61 +164,40 @@ def rank_program(g, core, T, topo):
     P.wait_ge(S.kq, 1)
     P.matmul_mx(T.ps_st[:, 0:256], T.Qc[:], T.Qs[:], T.Kc[:, 0:256], T.Ks[:, 0:256], True, True).then_inc(S.sta, 1)
     P.matmul_mx(T.ps_st[:, 512:768], T.Qc[:], T.Qs[:], T.Kc[:, 256:512], T.Ks[:, 256:512], True, True).then_inc(S.stb, 1)
-    for b in range(4):
-        P.matmul_mx(T.ps_s[:, 512 * b:512 * b + 128], T.Kc[:, 128 * b:128 * b + 128], T.Ks[:, 128 * b:128 * b + 128],
-                    T.Qc[:], T.Qs[:], True, True).then_inc(S["s%d" % b], 1)
-    for b in range(4):
-        AC.wait_ge(S["s%d" % b], 1)
-        AC.activation(T.t1[:, 128 * b:128 * b + 128], T.ps_s[:, 512 * b:512 * b + 128], ACTF.Identity,
-                      scale=A).then_inc(S["t%d" % b], 1)
-
     V.wait_ge(S.sta, 1)
     V.tensor_reduce(T.m2[:, 0:1], T.ps_st[:, 0:256], AxisListType.X, ALU.max).then_inc(S.m0, 1)
-    V.wait_ge(S.m0, 1)
-    V.tensor_scalar(T.m2[:, 2:3], T.m2[:, 0:1], A, None, ALU.mult).then_inc(S.m1, 1)
     V.wait_ge(S.stb, 1)
-    V.tensor_reduce(T.m2[:, 1:2], T.ps_st[:, 512:768], AxisListType.X, ALU.max).then_inc(S.m2, 1)
+    V.tensor_reduce(T.m2[:, 1:2], T.ps_st[:, 512:768], AxisListType.X, ALU.max).then_inc(S.m1, 1)
+    V.wait_ge(S.m0, 1)
     V.wait_ge(S.m1, 1)
-    V.wait_ge(S.m2, 1)
-    V.wait_ge(S.cst, 1)
-    V.tensor_scalar(T.xe[:], T.atile[:], T.m2[:, 1:2], T.m2[:, 2:3], ALU.mult, ALU.max).then_inc(S.xe, 1)
-    V.wait_ge(S.xe, 1)
-    V.transpose(T.xt[:, 0:32], T.xe[:]).then_inc(S.xt, 1)
-    V.wait_ge(S.xt, 1)
-    for a in range(1, 4):
-        V.tensor_copy(T.xt[0:1, 32 * a:32 * a + 32], T.xt[32 * a:32 * a + 1, 0:32]).then_inc(S.row, 1)
-    g.wait_ge(S.xt, 1)
-    g.wait_ge(S.row, 3)
-    g.partition_broadcast(T.cb[:], T.xt[0:1, 0:128], 128).then_inc(S.cb, 1)
-    SY.wait_ge(S.xt, 1)
-    SY.wait_ge(S.row, 3)
-    SY.dma_start(T.c[:], T.xt[0:1, 0:128]).then_inc(S.cout, 16)
-
+    V.tensor_scalar(T.negc[:, 0:1], T.m2[:, 1:2], T.m2[:, 0:1], -A, ALU.max, ALU.mult).then_inc(S.nc, 1)
+    V.wait_ge(S.nc, 1)
+    V.tensor_scalar(T.ccol[:, 0:1], T.negc[:, 0:1], -1.0, None, ALU.mult).then_inc(S.cc, 1)
     nxt = rrel.get(rank, root)
     if not is_root:
-        g.wait_ge(S.xe, 1)
-        loc += send(nxt, T.CL[:, rank:rank + 1], T.xe[:, 0:1], S.carr)
+        g.wait_ge(S.cc, 1)
+        loc += send(nxt, T.CL[:, rank:rank + 1], T.ccol[:, 0:1], S.carr)
 
-    V.wait_ge(S.cb, 1)
+    AC.wait_ge(S.nc, 1)
     for b in range(4):
-        V.wait_ge(S["t%d" % b], 1)
-        V.tensor_tensor(T.t1[:, 128 * b:128 * b + 128], T.t1[:, 128 * b:128 * b + 128], T.cb[:],
-                        ALU.subtract).then_inc(S["x%d" % b], 1)
-        AC.wait_ge(S["x%d" % b], 1)
-        AC.activation(T.e[:, 128 * b:128 * b + 128], T.t1[:, 128 * b:128 * b + 128], ACTF.Exp).then_inc(S["e%d" % b], 1)
-    V.wait_ge(S.fl, 1)
-    for b in range(4):
+        col = 512 * (b // 2) + 128 * (b % 2)
+        AC.activation(T.e[:, 128 * b:128 * b + 128], T.ps_st[:, col:col + 128], ACTF.Exp, bias=T.negc[:, 0:1],
+                      scale=A).then_inc(S["e%d" % b], 1)
         V.wait_ge(S["e%d" % b], 1)
-        V.tensor_scalar(T.pt[:, b:512:4], T.e[:, 128 * b:128 * b + 128], T.fl[:, 0:1], None, ALU.max).then_inc(S.pt, 1)
-    V.wait_ge(S.pt, 4)
+        V.transpose(T.X[:, b:512:4], T.e[:, 128 * b:128 * b + 128]).then_inc(S.tr, 1)
+    V.wait_ge(S.tr, 4)
+    V.wait_ge(S.fl, 1)
+    for a in range(4):
+        for c in range(4):
+            V.tensor_scalar(T.pt[32 * c:32 * c + 32, 128 * a:128 * a + 128], T.X[32 * a:32 * a + 32, 128 * c:128 * c + 128],
+                            T.fl[32 * a:32 * a + 32, 0:1], None, ALU.max).then_inc(S.pt, 1)
+    V.wait_ge(S.pt, 16)
     V.quantize_mx(T.Pc[:], T.Ps[:], T.pt[:]).then_inc(S.pq, 1)
-    SY.wait_ge(S.pt, 4)
-    SY.dma_start(T.p[:], T.pt[:]).then_inc(S.pout, 16)
 
     P.wait_ge(S.pq, 1)
     P.wait_ge(S.vq, 1)
     P.wait_ge(S.oneq, 1)
-    P.matmul_mx(T.ps_al[:, 0:130], T.Pc[:], T.Ps[:], T.VOc[:, 0:130], T.VOs[:, 0:130], True, True).then_inc(S.al, 1)
+    P.matmul_mx(T.ps_al[:, 0:256], T.Pc[:], T.Ps[:], T.VOc[:], T.VOs[:], True, True).then_inc(S.al, 1)
 
     if not is_root:
         V.wait_ge(S.al, 1)
@@ -222,19 +205,26 @@ def rank_program(g, core, T, topo):
         g.wait_ge(S.snd, 1)
         loc += send(nxt, slot(rank), T.snd[:, 0:AW], S["a%d" % rank])
         g.wait_ge(S.loc, loc)
-        SY.wait_ge(S.w0, 1)
-        for a in range(4):
-            SY.dma_start(T.w[0:N, 32 * a:32 * a + 32], T.W[0:N, 0:32]).then_inc(S.wout, 16)
+        SY.wait_ge(S.loc, loc)
+        SY.wait_ge(S.pt, 16)
+        SY.dma_start(T.p[:], T.pt[:]).then_inc(S.pout, 16)
+        SY.wait_ge(S.cc, 1)
+        SY.dma_start(T.c[:], T.ccol[:, 0:1]).then_inc(S.cout, 16)
         SY.wait_ge(S.cout, 16)
         SY.wait_ge(S.pout, 16)
-        SY.wait_ge(S.wout, 64)
+        SY.wait_ge(S.wout, 16)
         return
 
+    SY.wait_ge(S.pt, 16)
+    SY.dma_start(T.p[:], T.pt[:]).then_inc(S.pout, 16)
+    SY.wait_ge(S.cc, 1)
+    SY.dma_start(T.c[:], T.ccol[:, 0:1]).then_inc(S.cout, 16)
     others = [j for j in range(N) if j != rootr]
     near = [j for j in others if j not in rrel]
     far = [j for j in others if j in rrel]
     ncarr = sum(_nb(topo.mask(rrel.get(j, cores[j]), core)) for j in others)
-    V.tensor_copy(T.C6[:, rootr:rootr + 1], T.xe[:, 0:1]).then_inc(S.c6, 1)
+    V.wait_ge(S.cc, 1)
+    V.tensor_copy(T.C6[:, rootr:rootr + 1], T.ccol[:, 0:1]).then_inc(S.c6, 1)
     V.wait_ge(S.carr, ncarr)
     V.tensor_copy(T.C6[:, 0:N - 1], T.CL[:, 0:N - 1]).then_inc(S.c6, 1)
     V.wait_ge(S.c6, 2)

import numpy as np
from concourse.bass import DstId, RemoteDMATransfer
from concourse.mybir import dt, AluOpType, AxisListType, ActivationFunctionType

NSIM = 256
N, NQ = 6, 128
A = float(np.float32(0.0125))
AW, SLOT = 129, 132
NT = 5
F32, BF, CODE, U8 = "float32", "bfloat16", "float8_e4m3fn_x4", "uint8"

SCRATCH = {
    "qt": ("sbuf", [128, 512], BF), "kt": ("sbuf", [128, 2048], BF), "vt": ("sbuf", [128, 512], BF),
    "onet": ("sbuf", [128, 512], BF),
    "Qc": ("sbuf", [128, 128], CODE), "Qs": ("sbuf", [128, 128], U8),
    "Kc": ("sbuf", [128, 512], CODE), "Ks": ("sbuf", [128, 512], U8),
    "VOc": ("sbuf", [128, 256], CODE), "VOs": ("sbuf", [128, 256], U8),
    "Pc": ("sbuf", [128, 128], CODE), "Ps": ("sbuf", [128, 128], U8),
    "ps_st": ("psum", [128, 1024], F32), "ps_al": ("psum", [128, 512], F32),
    "n20": ("sbuf", [128, 1], F32), "fl": ("sbuf", [128, 1], BF),
    "m2": ("sbuf", [128, 4], F32), "negc": ("sbuf", [128, 4], F32), "ccol": ("sbuf", [128, 4], F32),
    "zw": ("sbuf", [128, 128], F32),
    "e": ("sbuf", [128, 512], BF), "X": ("sbuf", [128, 512], BF),
    "pt": ("sbuf", [128, 512], BF), "snd": ("sbuf", [128, SLOT], F32),
    "CL": ("sbuf", [128, 8], F32), "G": ("sbuf", [128, 5 * SLOT], F32),
    "C6": ("sbuf", [128, 8], F32), "negM": ("sbuf", [128, 1], F32),
    "W": ("sbuf", [128, 32], F32), "WT": ("sbuf", [128, 32], F32),
    "ta": ("sbuf", [128, SLOT], F32), "tb": ("sbuf", [128, SLOT], F32),
    "YB": ("sbuf", [128, NT * AW], F32), "RHO": ("sbuf", [128, NT * AW], F32), "Z": ("sbuf", [128, NT * AW], F32),
    "r": ("sbuf", [128, 1], F32), "XB": ("sbuf", [128, 128], F32), "O": ("sbuf", [128, 128], F32),
}
SEMAPHORES = ["q", "k", "v", "one", "n20", "fl", "w0", "oneq", "qq", "vq", "kq", "qs", "qc", "loc",
              "sta", "stb", "m0", "m1", "nc", "cc", "zw", "tr",
              "e0", "e1", "e2", "e3", "pt", "pq", "al", "snd",
              "carr", "a0", "a1", "a2", "a3", "a4", "c6", "nm", "w", "wt", "ya", "yb", "y", "rho1", "rho2",
              "z", "r", "xb", "o", "cout", "pout", "wout", "oout"]


def _nb(mask):
    return bin(mask).count("1")


def _chip_cores(topo, c):
    return [x for x in range(NSIM) if topo.host(x) == topo.host(c) and topo.chip(x) == topo.chip(c) and x != c]


def _plan(T, topo):
    cores = list(T.cores)
    root = cores[T.root]
    qrel, rrel = {}, {}
    for j in range(N):
        if j == T.root:
            continue
        if not topo.may_write(root, cores[j]):
            cand = [x for x in _chip_cores(topo, root) if topo.may_write(x, cores[j])]
            qrel[j] = cand[len(qrel) % len(cand)]
        if not topo.may_write(cores[j], root):
            cand = [x for x in _chip_cores(topo, cores[j]) if topo.may_write(x, root)]
            rrel[j] = cand[(len(rrel) + len(cand) // 2) % len(cand)]
    return qrel, rrel


def rank_program(g, core, T, topo):
    S = T.sem
    cores = list(T.cores)
    rootr = T.root
    root = cores[rootr]
    qrel, rrel = _plan(T, topo)
    rank = T.rank_of(core)
    ALU, ACTF = AluOpType, ActivationFunctionType
    u8 = dt.uint8

    def send(dst, out, in_, rsem):
        rid, pid = topo.addr(dst, core)
        m = topo.mask(core, dst)
        g.remote_dma(out_ap=out, in_ap=in_, remote_sem=rsem, local_sem=S.loc, pid=pid, routing_id=rid,
                     dma_engine_mask=m)
        return _nb(m)

    def slot(j):
        return T.G[:, SLOT * j:SLOT * j + AW]

    if rank is None:
        loc = 0
        mine = [j for j in qrel if qrel[j] == core]
        if mine:
            nin = _nb(topo.mask(root, core))
            g.wait_ge(S.qs, nin)
            for j in mine:
                loc += send(cores[j], T.Qs[:], T.Qs[:], S.qs)
            g.wait_ge(S.qc, nin)
            for j in mine:
                loc += send(cores[j], T.Qc[:].bitcast(u8), T.Qc[:].bitcast(u8), S.qc)
        for j in [j for j in rrel if rrel[j] == core]:
            nin = _nb(topo.mask(cores[j], core))
            g.wait_ge(S.carr, nin)
            loc += send(root, T.CL[:, j:j + 1], T.CL[:, j:j + 1], S.carr)
            g.wait_ge(S["a%d" % j], nin)
            loc += send(root, slot(j), slot(j), S["a%d" % j])
        if loc:
            g.wait_ge(S.loc, loc)
        return

    V, P, AC, SY = g.vector, g.tensor, g.scalar, g.sync
    is_root = rank == rootr

    if is_root:
        SY.dma_start(T.qt[:], T.q[:]).then_inc(S.q, 16)
    else:
        SY.dma_start(T.kt[:], T.k[:]).then_inc(S.k, 16)
        AC.dma_start(T.vt[:], T.v[:]).then_inc(S.v, 16)

    V.memset(T.onet[:], 1.0).then_inc(S.one, 1)
    V.memset(T.n20[:], -20.0).then_inc(S.n20, 1)
    if is_root:
        V.memset(T.W[:], 0.0).then_inc(S.w0, 1)
        V.wait_ge(S.q, 16)
        V.quantize_mx(T.Qc[:], T.Qs[:], T.qt[:]).then_inc(S.qq, 1)
        V.memset(T.RHO[:], 1.0).then_inc(S.rho1, 1)
        V.wait_ge(S.rho1, 1)
        V.tensor_scalar(T.RHO[:, 0:NT * AW:NT], T.RHO[:, 0:NT * AW:NT], 0.0, None, ALU.mult).then_inc(S.rho2, 1)
    else:
        V.memset(T.zw[:], 0.0).then_inc(S.zw, 1)
        SY.wait_ge(S.zw, 1)
        SY.dma_start(T.w[:], T.zw[0:N, 0:NQ]).then_inc(S.wout, 16)
    V.wait_ge(S.one, 1)
    V.quantize_mx(T.VOc[:, 128:256], T.VOs[:, 128:256], T.onet[:]).then_inc(S.oneq, 1)
    V.wait_ge(S.k, 16)
    V.quantize_mx(T.Kc[:], T.Ks[:], T.kt[:]).then_inc(S.kq, 1)
    V.wait_ge(S.v, 16)
    V.quantize_mx(T.VOc[:, 0:128], T.VOs[:, 0:128], T.vt[:]).then_inc(S.vq, 1)

    AC.wait_ge(S.n20, 1)
    AC.activation(T.fl[:], T.n20[:], ACTF.Exp).then_inc(S.fl, 1)

    loc = 0
    if is_root:
        g.wait_ge(S.qq, 1)
        rel = [qrel[j] for j in sorted(qrel)]
        if rel:
            m = topo.mask(core, rel[0])
            for x in rel:
                m &= topo.mask(core, x)
            ids = [DstId(rid=topo.addr(x, core)[0], pnc=topo.addr(x, core)[1]) for x in rel]
            g.remote_dma_fused([RemoteDMATransfer(dst_ids=ids, dma_engine_mask=m, remote_sem=S.qs, srcs=[T.Qs[:]],
                                                  dsts=[T.Qs[:] for x in rel])], local_sem=S.loc)
            g.remote_dma_fused([RemoteDMATransfer(dst_ids=ids, dma_engine_mask=m, remote_sem=S.qc,
                                                  srcs=[T.Qc[:].bitcast(u8)],
                                                  dsts=[T.Qc[:].bitcast(u8) for x in rel])], local_sem=S.loc)
            loc += 2 * _nb(m)
        for j in range(N):
            if j != rootr and j not in qrel:
                loc += send(cores[j], T.Qs[:], T.Qs[:], S.qs)
                loc += send(cores[j], T.Qc[:].bitcast(u8), T.Qc[:].bitcast(u8), S.qc)
        SY.wait_ge(S.loc, loc)
        SY.dma_start(T.kt[:], T.k[:]).then_inc(S.k, 16)
        SY.dma_start(T.vt[:], T.v[:]).then_inc(S.v, 16)
        P.wait_ge(S.qq, 1)
    else:
        nin = _nb(topo.mask(qrel.get(rank, root), core))
        P.wait_ge(S.qs, nin)
        P.wait_ge(S.qc, nin)

    P.wait_ge(S.kq, 1)
    P.matmul_mx(T.ps_st[:, 0:256], T.Qc[:], T.Qs[:], T.Kc[:, 0:256], T.Ks[:, 0:256], True, True).then_inc(S.sta, 1)
    P.matmul_mx(T.ps_st[:, 512:768], T.Qc[:], T.Qs[:], T.Kc[:, 256:512], T.Ks[:, 256:512], True, True).then_inc(S.stb, 1)
    V.wait_ge(S.sta, 1)
    V.tensor_reduce(T.m2[:, 0:1], T.ps_st[:, 0:256], AxisListType.X, ALU.max).then_inc(S.m0, 1)
    V.wait_ge(S.stb, 1)
    V.tensor_reduce(T.m2[:, 1:2], T.ps_st[:, 512:768], AxisListType.X, ALU.max).then_inc(S.m1, 1)
    V.wait_ge(S.m0, 1)
    V.wait_ge(S.m1, 1)
    V.tensor_scalar(T.negc[:, 0:1], T.m2[:, 1:2], T.m2[:, 0:1], -A, ALU.max, ALU.mult).then_inc(S.nc, 1)
    V.wait_ge(S.nc, 1)
    V.tensor_scalar(T.ccol[:, 0:1], T.negc[:, 0:1], -1.0, None, ALU.mult).then_inc(S.cc, 1)
    nxt = rrel.get(rank, root)
    if not is_root:
        g.wait_ge(S.cc, 1)
        loc += send(nxt, T.CL[:, rank:rank + 1], T.ccol[:, 0:1], S.carr)

    AC.wait_ge(S.nc, 1)
    for b in range(4):
        col = 512 * (b // 2) + 128 * (b % 2)
        AC.activation(T.e[:, 128 * b:128 * b + 128], T.ps_st[:, col:col + 128], ACTF.Exp, bias=T.negc[:, 0:1],
                      scale=A).then_inc(S["e%d" % b], 1)
        V.wait_ge(S["e%d" % b], 1)
        V.transpose(T.X[:, b:512:4], T.e[:, 128 * b:128 * b + 128]).then_inc(S.tr, 1)
    V.wait_ge(S.tr, 4)
    V.wait_ge(S.fl, 1)
    for a in range(4):
        for c in range(4):
            V.tensor_scalar(T.pt[32 * c:32 * c + 32, 128 * a:128 * a + 128], T.X[32 * a:32 * a + 32, 128 * c:128 * c + 128],
                            T.fl[32 * a:32 * a + 32, 0:1], None, ALU.max).then_inc(S.pt, 1)
    V.wait_ge(S.pt, 16)
    V.quantize_mx(T.Pc[:], T.Ps[:], T.pt[:]).then_inc(S.pq, 1)

    P.wait_ge(S.pq, 1)
    P.wait_ge(S.vq, 1)
    P.wait_ge(S.oneq, 1)
    P.matmul_mx(T.ps_al[:, 0:256], T.Pc[:], T.Ps[:], T.VOc[:], T.VOs[:], True, True).then_inc(S.al, 1)

    if not is_root:
        V.wait_ge(S.al, 1)
        V.tensor_copy(T.snd[:, 0:AW], T.ps_al[:, 0:AW]).then_inc(S.snd, 1)
        g.wait_ge(S.snd, 1)
        loc += send(nxt, slot(rank), T.snd[:, 0:AW], S["a%d" % rank])
        g.wait_ge(S.loc, loc)
        SY.wait_ge(S.loc, loc)
        SY.wait_ge(S.pt, 16)
        SY.dma_start(T.p[:], T.pt[:]).then_inc(S.pout, 16)
        SY.wait_ge(S.cc, 1)
        SY.dma_start(T.c[:], T.ccol[:, 0:1]).then_inc(S.cout, 16)
        SY.wait_ge(S.cout, 16)
        SY.wait_ge(S.pout, 16)
        SY.wait_ge(S.wout, 16)
        return

    SY.wait_ge(S.pt, 16)
    SY.dma_start(T.p[:], T.pt[:]).then_inc(S.pout, 16)
    SY.wait_ge(S.cc, 1)
    SY.dma_start(T.c[:], T.ccol[:, 0:1]).then_inc(S.cout, 16)
    others = [j for j in range(N) if j != rootr]
    near = [j for j in others if j not in rrel]
    far = [j for j in others if j in rrel]
    ncarr = sum(_nb(topo.mask(rrel.get(j, cores[j]), core)) for j in others)
    V.wait_ge(S.cc, 1)
    V.tensor_copy(T.C6[:, rootr:rootr + 1], T.ccol[:, 0:1]).then_inc(S.c6, 1)
    V.wait_ge(S.carr, ncarr)
    V.tensor_copy(T.C6[:, 0:N - 1], T.CL[:, 0:N - 1]).then_inc(S.c6, 1)
    V.wait_ge(S.c6, 2)
    V.tensor_reduce(T.negM[:], T.C6[:, 0:N], AxisListType.X, ALU.max, negate=True).then_inc(S.nm, 1)
    AC.wait_ge(S.nm, 1)
    AC.wait_ge(S.c6, 2)
    AC.wait_ge(S.w0, 1)
    AC.activation(T.W[:, 0:N], T.C6[:, 0:N], ACTF.Exp, bias=T.negM[:, 0:1]).then_inc(S.w, 1)
    AC.wait_ge(S.w, 1)
    V.wait_ge(S.w, 1)
    V.wait_ge(S.w0, 1)
    V.transpose(T.WT[:], T.W[:]).then_inc(S.wt, 1)
    SY.wait_ge(S.wt, 1)
    for a in range(4):
        SY.dma_start(T.w[0:N, 32 * a:32 * a + 32], T.WT[32 * a:32 * a + N, 0:32]).then_inc(S.wout, 16)

    def arrived(q, j):
        q.wait_ge(S["a%d" % j], _nb(topo.mask(rrel.get(j, cores[j]), core)))

    V.wait_ge(S.al, 1)
    V.tensor_scalar(T.ta[:, 0:AW], T.ps_al[:, 0:AW], T.W[:, rootr:rootr + 1], None, ALU.mult).then_inc(S.ya, 1)
    j = near[0]
    arrived(AC, j)
    AC.activation(T.tb[:, 0:AW], slot(j), ACTF.Identity, scale=T.W[:, j:j + 1]).then_inc(S.yb, 1)
    V.wait_ge(S.ya, 1)
    V.wait_ge(S.yb, 1)
    V.tensor_tensor(T.YB[:, 0:NT * AW:NT], T.ta[:, 0:AW], T.tb[:, 0:AW], ALU.add).then_inc(S.y, 1)
    for i, j in enumerate(far):
        out = T.YB[:, i + 1:NT * AW:NT]
        if i % 2 == 0:
            arrived(AC, j)
            AC.activation(out, slot(j), ACTF.Identity, scale=T.W[:, j:j + 1]).then_inc(S.y, 1)
        else:
            arrived(V, j)
            V.tensor_scalar(out, slot(j), T.W[:, j:j + 1], None, ALU.mult).then_inc(S.y, 1)
    V.wait_ge(S.y, NT)
    V.wait_ge(S.rho2, 1)
    V.tensor_tensor_scan(T.Z[:], T.RHO[:], T.YB[:], 0.0, ALU.mult, ALU.add).then_inc(S.z, 1)
    V.wait_ge(S.z, 1)
    V.reciprocal(T.r[:], T.Z[:, NT * AW - 1:NT * AW]).then_inc(S.r, 1)
    V.wait_ge(S.r, 1)
    AC.wait_ge(S.z, 1)
    AC.wait_ge(S.r, 1)
    n = 0
    for a in range(4):
        for b in range(4):
            in0 = T.Z[32 * a:32 * a + 32, NT * 32 * b + NT - 1:NT * 32 * (b + 1):NT]
            out = T.XB[32 * b:32 * b + 32, 32 * a:32 * a + 32]
            sc = T.r[32 * a:32 * a + 32, 0:1]
            if n % 2 == 0:
                V.tensor_scalar(out, in0, sc, None, ALU.mult).then_inc(S.xb, 1)
            else:
                AC.activation(out, in0, ACTF.Identity, scale=sc).then_inc(S.xb, 1)
            n += 1
    V.wait_ge(S.xb, 16)
    V.transpose(T.O[:], T.XB[:]).then_inc(S.o, 1)
    SY.wait_ge(S.o, 1)
    SY.dma_start(T.o[:], T.O[:]).then_inc(S.oout, 16)
    g.wait_ge(S.loc, loc)
    SY.wait_ge(S.cout, 16)
    SY.wait_ge(S.pout, 16)
    SY.wait_ge(S.wout, 64)
    SY.wait_ge(S.oout, 16)
